import numpy as np
import ml_dtypes


def mxq(x, axis, fmt="e4m3"):
    dtype, down = {"e4m3": (ml_dtypes.float8_e4m3fn, 7), "e5m2": (ml_dtypes.float8_e5m2, 14)}[fmt]
    v = np.moveaxis(np.asarray(x, np.float32).astype(ml_dtypes.bfloat16).astype(np.float64), axis, -1)
    blocks = v.reshape(v.shape[:-1] + (-1, 32))
    amax = np.abs(blocks).max(-1, keepdims=True)
    byte = np.maximum(np.where(amax > 0, np.frexp(amax)[1] - 1 + 127, 0) - down, 1)
    scale = np.exp2(byte - 127.0)
    codes = (blocks / scale).astype(np.float32).astype(dtype).astype(np.float64)
    return np.moveaxis((codes * scale).reshape(v.shape), -1, axis)


WIDE = False


def mx_kscale(k):
    if not WIDE:
        return np.ones(k)
    levels = np.array([10, -10, 5, -5, 0])
    if k % 512:
        return np.exp2(np.random.permutation(np.resize(levels, k // 32))).repeat(32)
    a = np.empty((k // 512, 16))
    for p in range(k // 512):
        a[p, :8] = np.random.permutation(np.resize(levels, 8))
        for g in range(8):
            far = levels[np.abs(levels - a[p, g]) >= 10]
            a[p, g + 8] = far[np.random.randint(len(far))]
    return np.exp2(a.ravel()).repeat(32)


BF16 = ml_dtypes.bfloat16


def bf(x):
    return np.asarray(x, np.float32).astype(BF16)


def f64(x):
    return np.asarray(x).astype(np.float64)

E4M3FN = np.array([(-1.0 if i & 128 else 1.0) * ((1.0 + (i & 7) / 8.0) * 2.0 ** (((i >> 3) & 15) - 7) if i & 120 else (i & 7) * 2.0 ** -9) for i in range(256)])


def e4m3fn_bytes(y):
    return np.clip(np.asarray(y, np.float64), -448.0, 448.0).astype(np.float32).astype(ml_dtypes.float8_e4m3fn).view(np.uint8)


def e4m3fn_values(b):
    return E4M3FN[b]


Z, V, R, B = 1024, 2048, 1536, 512

FP8_MAX = 448.0
DEPTH = 0.6


def setup_inputs():
    s = mx_kscale(V)
    t = mx_kscale(R)
    footprint = np.random.uniform(0.5, 1.5, (V, 1))
    S = np.random.standard_normal((V, R)) * footprint * DEPTH / np.sqrt(V) * s[:, None]
    S_scale = (np.abs(S).max(axis=1, keepdims=True) / FP8_MAX).astype(np.float32)
    S_bytes = e4m3fn_bytes(S / f64(S_scale))
    F = np.random.standard_normal((Z, V)) / s
    i0 = np.random.uniform(0.5, 1.5, R) * t
    D = np.random.standard_normal((R, B)) / np.sqrt(R) / t[:, None]
    return {"F": bf(F), "S_bytes": S_bytes, "S_scale": S_scale, "i0": bf(i0), "D": bf(D)}


def reference(F, S_bytes, S_scale, i0, D):
    S = e4m3fn_values(S_bytes) * np.repeat(f64(S_scale), R, axis=1)
    p = mxq(f64(F), 1, "e4m3") @ mxq(S, 0, "e4m3")
    h = f64(i0) * np.exp(-p)
    y = mxq(h, 1, "e4m3") @ mxq(f64(D), 0, "e4m3")
    return y

@@ -1,0 +1,362 @@
+from contextlib import ExitStack
+
+import concourse.mybir as mybir
+from concourse.masks import make_identity
+
+Z, V, R, B = 1024, 2048, 1536, 512
+FLOPS = 2 * Z * V * R + 2 * Z * R * B
+
+F32 = mybir.dt.float32
+BF16 = mybir.dt.bfloat16
+U32 = mybir.dt.uint32
+U8 = mybir.dt.uint8
+FP8 = mybir.dt.float8_e4m3fn
+FP8X4 = mybir.dt.float8_e4m3fn_x4
+ALU = mybir.AluOpType
+ACT = mybir.ActivationFunctionType
+
+P = 128
+PACK = 4
+KP = 512
+G = V // KP
+C = R // KP
+ZH = 512
+NH = Z // ZH
+
+
+def tile_tomography_forward_transmission_d3_kernel(tc, F, S_bytes, S_scale, i0, D, out):
+    nc = tc.nc
+    with ExitStack() as ctx:
+        keep = ctx.enter_context(tc.tile_pool(name="keep", bufs=1))
+        fraw_pool = ctx.enter_context(tc.tile_pool(name="fraw", bufs=5))
+        grp = ctx.enter_context(tc.tile_pool(name="grp", bufs=4))
+        big = ctx.enter_context(tc.tile_pool(name="big", bufs=4))
+        sq = ctx.enter_context(tc.tile_pool(name="sq", bufs=8))
+        hp = ctx.enter_context(tc.tile_pool(name="hp", bufs=2))
+        hq = ctx.enter_context(tc.tile_pool(name="hq", bufs=1))
+        psum = ctx.enter_context(tc.psum_pool(name="psum", bufs=8))
+        ctx.enter_context(tc.manual_schedule())
+
+        scale = keep.tile([P, G, PACK], F32, name="scale")
+        i0_t = keep.tile([P, C, PACK], BF16, name="i0_t")
+        nc.scalar.dma_start(out=scale[:], in_=S_scale.rearrange("(g p t) o -> p g (t o)", p=P, t=PACK))
+        nc.scalar.dma_start(out=i0_t[:], in_=i0.rearrange("(c p t) -> p c t", p=P, t=PACK))
+        s_view = S_bytes.rearrange("(g p t) n -> g p t n", p=P, t=PACK)
+        sb_a, sb_b = [], []
+        for g in range(G):
+            a = keep.tile([P, PACK, KP], U8, name="s_bytes_a%d" % g)
+            b = keep.tile([P, PACK, 2 * KP], U8, name="s_bytes_b%d" % g)
+            sb_a.append(a)
+            sb_b.append(b)
+        f_raw = {}
+        d_raw = []
+        for c in range(C):
+            dr = keep.tile([P, PACK, B], BF16, name="d_raw%d" % c)
+            d_raw.append(dr)
+
+        def load_f(z):
+            fr = fraw_pool.tile([P, V], BF16, name="f_raw")
+            f_raw[z] = fr
+            nc.sync.dma_start(out=fr[:], in_=F[P * z : P * (z + 1), :])
+
+        d_view = D.rearrange("(c p t) b -> c p t b", p=P, t=PACK)
+
+        def load_sa(g):
+            nc.sync.dma_start(out=sb_a[g][:], in_=s_view[g][:, :, 0:KP])
+
+        def load_sb(g):
+            nc.sync.dma_start(out=sb_b[g][:], in_=s_view[g][:, :, KP:R])
+
+        def load_d(c):
+            nc.sync.dma_start(out=d_raw[c][:], in_=d_view[c])
+
+
+        ident = keep.tile([P, P], F32, name="ident")
+        make_identity(nc, ident[:])
+
+        i0_flat = i0_t[:].rearrange("p c t -> p (c t)")
+        neg = keep.tile([P, C * PACK], F32, name="neg")
+        mag = keep.tile([P, C * PACK], F32, name="mag")
+        fac = keep.tile([P, 2, C * PACK], F32, name="fac")
+        inv = keep.tile([P, C * PACK], F32, name="inv")
+        lnf = keep.tile([P, 2, C * PACK], F32, name="lnf")
+        ln_i0 = keep.tile([P, C * PACK], F32, name="ln_i0")
+        sgn = keep.tile([P, C * PACK], F32, name="sgn")
+
+        def prep_a():
+            nc.vector.tensor_scalar(out=neg[:], in0=i0_flat, scalar1=-1.0, scalar2=None, op0=ALU.mult)
+            nc.vector.tensor_tensor(out=mag[:], in0=i0_flat, in1=neg[:], op=ALU.max)
+            nc.vector.tensor_scalar(out=mag[:], in0=mag[:], scalar1=2.0**-126, scalar2=None, op0=ALU.max)
+            nc.vector.tensor_scalar(out=fac[:, 0, :], in0=mag[:], scalar1=2.0**-63, scalar2=2.0**64, op0=ALU.max, op1=ALU.min)
+            nc.vector.reciprocal(out=inv[:], in_=fac[:, 0, :])
+            nc.vector.tensor_tensor(out=fac[:, 1, :], in0=mag[:], in1=inv[:], op=ALU.mult)
+            nc.scalar.activation(out=lnf[:], in_=fac[:], func=ACT.Ln)
+
+        def prep_b():
+            nc.vector.tensor_tensor(out=ln_i0[:], in0=lnf[:, 0, :], in1=lnf[:, 1, :], op=ALU.add)
+            nc.vector.tensor_scalar(out=sgn[:], in0=i0_flat, scalar1=0.0, scalar2=2.0, op0=ALU.is_ge, op1=ALU.mult)
+            nc.vector.tensor_scalar(out=sgn[:], in0=sgn[:], scalar1=-1.0, scalar2=None, op0=ALU.add)
+
+        s_wide = {}
+
+        def new_wide(c):
+            wide_tile = big.tile([P, PACK, G * KP], BF16, name="big", align_bytes=64)
+            s_wide[c] = wide_tile
+        s_grp, s_codes, s_scales = {}, {}, {}
+
+        def widen(c, g, j, eng):
+            src = sb_a[g][:, j, :] if c == 0 else sb_b[g][:, j, KP * (c - 1) : KP * c]
+            dst = s_wide[c][:, j, KP * g : KP * (g + 1)]
+            if eng == "v":
+                nc.vector.tensor_scalar(out=dst, in0=src.bitcast(FP8), scalar1=scale[:, g, j : j + 1], scalar2=None, op0=ALU.mult)
+            else:
+                nc.scalar.activation(out=dst, in_=src.bitcast(FP8), func=ACT.Copy, scale=scale[:, g, j : j + 1])
+
+        def s_inter(c, t):
+            gt = grp.tile([P, 4 * KP], BF16, name="s_grp", align_bytes=64)
+            s_grp[c, t] = gt
+            src = s_wide[c][:].rearrange("p j (q i t) -> p t q j i", i=4, t=4)
+            dst = gt[:].rearrange("p (q i j) -> p q j i", i=4, j=4)
+            nc.vector.tensor_copy(out=dst, in_=src[:, t])
+
+        def s_quant(c, t):
+            co = sq.tile([P, KP], U32, name="s_codes", align_bytes=64)
+            sc = sq.tile([P, KP], U8, name="s_scales", align_bytes=64)
+            s_codes[c, t], s_scales[c, t] = co, sc
+            nc.vector.quantize_mx(out=co[:].bitcast(FP8X4), scales=sc[:], in_=s_grp[c, t][:])
+
+        f_grp = {}
+
+        def new_f_grp(h):
+            f_grp_tile = big.tile([P, G, ZH * 2], F32, name="big", align_bytes=64)
+            f_grp[h] = f_grp_tile
+        f_codes = [keep.tile([P, G, ZH], U32, name="f_codes%d" % h, align_bytes=64) for h in range(NH)]
+        f_scales = [keep.tile([P, G, ZH], U8, name="f_scales%d" % h, align_bytes=64) for h in range(NH)]
+
+        def f_turn(z):
+            words = f_raw[z][:].bitcast(F32)
+            h, zz = divmod(z, 4)
+            for gp in range(2):
+                bank = psum.tile([P, 512], F32, name="bank")
+                for k in range(2):
+                    for u in range(2):
+                        g = 2 * gp + k
+                        nc.tensor.transpose(
+                            bank[:, (2 * k + u) * P : (2 * k + u + 1) * P],
+                            words[:, 256 * g + u : 256 * (g + 1) : 2],
+                            ident[:],
+                        )
+                dst = f_grp[h][:, 2 * gp : 2 * gp + 2, 2 * P * zz : 2 * P * (zz + 1)]
+                nc.scalar.copy(
+                    out=dst.rearrange("p g (r u) -> p g r u", u=2),
+                    in_=bank[:].rearrange("p (g u r) -> p g r u", g=2, u=2),
+                )
+
+        def f_quant(h, g):
+            nc.vector.quantize_mx(
+                out=f_codes[h][:, g, :].bitcast(FP8X4), scales=f_scales[h][:, g, :], in_=f_grp[h][:, g, :].bitcast(BF16)
+            )
+
+        h_planes = {}
+        banks = {}
+
+        def project(c, t, h):
+            bank = psum.tile([P, 512], F32, name="bank")
+            banks[c, t, h] = bank
+            for g in range(G):
+                cols = slice(P * g, P * (g + 1))
+                nc.tensor.matmul_mx(
+                    out=bank[:],
+                    lhsT=s_codes[c, t][:, cols].bitcast(FP8X4),
+                    lhsT_scale=s_scales[c, t][:, cols],
+                    rhs=f_codes[h][:, g, :].bitcast(FP8X4),
+                    rhs_scale=f_scales[h][:, g, :],
+                    start=(g == 0),
+                    stop=(g == G - 1),
+                )
+
+        def attenuate(c, t, h):
+            if c not in h_planes:
+                h_planes[c] = hp.tile([P, PACK, Z], BF16, name="h_plane", align_bytes=64)
+            nc.scalar.activation(
+                out=h_planes[c][:, t, ZH * h : ZH * (h + 1)],
+                in_=banks[c, t, h][:],
+                func=ACT.Exp,
+                bias=ln_i0[:, PACK * c + t : PACK * c + t + 1],
+                scale=-1.0,
+            )
+
+        h_grp = {}
+        h_codes = [hq.tile([P, Z], U32, name="h_codes%d" % c, align_bytes=64) for c in range(C)]
+        h_scales = [hq.tile([P, Z], U8, name="h_scales%d" % c, align_bytes=64) for c in range(C)]
+
+        def h_inter(c, z0, w):
+            gt = grp.tile([P, 4 * KP], BF16, name="s_grp", align_bytes=64)
+            h_grp[c, z0] = gt
+            src = h_planes[c][:, :, z0 : z0 + w].rearrange("p j (q i) -> p q j i", i=4)
+            dst = gt[:, 0 : 4 * w].rearrange("p (q i j) -> p q j i", i=4, j=4)
+            nc.vector.tensor_copy(out=dst, in_=src)
+
+        def h_quant(c, z0, w):
+            nc.vector.quantize_mx(
+                out=h_codes[c][:, z0 : z0 + w].bitcast(FP8X4), scales=h_scales[c][:, z0 : z0 + w], in_=h_grp[c, z0][:, 0 : 4 * w]
+            )
+
+        d_grp = []
+        d_codes = [keep.tile([P, B], U32, name="d_codes%d" % c, align_bytes=64) for c in range(C)]
+        d_scales = [keep.tile([P, B], U8, name="d_scales%d" % c, align_bytes=64) for c in range(C)]
+
+        def d_sign(c):
+            for j in range(PACK):
+                nc.vector.tensor_scalar(
+                    out=d_raw[c][:, j, :], in0=d_raw[c][:, j, :], scalar1=sgn[:, PACK * c + j : PACK * c + j + 1], scalar2=None, op0=ALU.mult
+                )
+
+        def d_inter(c, eng="v"):
+            if not d_grp:
+                d_grp_tile = big.tile([P, C, PACK * B], BF16, name="big", align_bytes=64)
+                d_grp.append(d_grp_tile)
+            dst = d_grp[0][:, c, :].rearrange("p (q i j) -> p q j i", i=4, j=4)
+            src = d_raw[c][:].rearrange("p j (q i) -> p q j i", i=4)
+            if eng == "v":
+                nc.vector.tensor_copy(out=dst, in_=src)
+            else:
+                nc.scalar.copy(out=dst, in_=src)
+
+        def d_quant(c):
+            nc.vector.quantize_mx(out=d_codes[c][:].bitcast(FP8X4), scales=d_scales[c][:], in_=d_grp[0][:, c, :])
+
+        y_banks = {}
+        y_all = []
+
+        def detect(z, cs):
+            if z not in y_banks:
+                y_banks[z] = psum.tile([P, 512], F32, name="bank")
+            for c in cs:
+                cols = slice(P * z, P * (z + 1))
+                nc.tensor.matmul_mx(
+                    out=y_banks[z][:],
+                    lhsT=h_codes[c][:, cols].bitcast(FP8X4),
+                    lhsT_scale=h_scales[c][:, cols],
+                    rhs=d_codes[c][:].bitcast(FP8X4),
+                    rhs_scale=d_scales[c][:],
+                    start=(c == 0),
+                    stop=(c == C - 1),
+                )
+
+        def store(z, eng):
+            if not y_all:
+                y_tile = big.tile([P, 8, B], F32, name="big", align_bytes=64)
+                y_all.append(y_tile)
+            yt = y_all[0][:, z, :]
+            if eng == "v":
+                nc.vector.tensor_copy(out=yt, in_=y_banks[z][:])
+            else:
+                nc.scalar.copy(out=yt, in_=y_banks[z][:])
+            nc.sync.dma_start(out=out[P * z : P * (z + 1), :], in_=yt)
+
+        for g in range(G):
+            load_sa(g)
+        for z in range(5):
+            load_f(z)
+        new_f_grp(0)
+        new_wide(0)
+        new_f_grp(1)
+        new_wide(1)
+        for j in range(PACK):
+            widen(0, 0, j, "s" if j >= 2 else "v")
+        prep_a()
+        for g in range(1, G):
+            for j in range(PACK):
+                widen(0, g, j, "s" if j >= (2 if g < 2 else 3) else "v")
+        prep_b()
+        for z in range(4):
+            f_turn(z)
+        for z in range(5, 8):
+            load_f(z)
+        for g in range(G):
+            load_sb(g)
+        for c in range(C):
+            load_d(c)
+        s_inter(0, 0)
+        s_inter(0, 1)
+        s_quant(0, 0)
+        s_quant(0, 1)
+        s_inter(0, 2)
+        for g in range(G):
+            f_quant(0, g)
+        s_inter(0, 3)
+        s_quant(0, 2)
+        s_quant(0, 3)
+        for z in range(4, 8):
+            f_turn(z)
+        for t in range(4):
+            project(0, t, 0)
+        for g in range(G):
+            for j in range(2):
+                widen(1, g, j, "v")
+        for g in range(G):
+            f_quant(1, g)
+        for t in range(4):
+            project(0, t, 1)
+        for g in range(G):
+            for j in range(2, PACK):
+                widen(1, g, j, "s")
+        for h in range(NH):
+            for t in range(4):
+                attenuate(0, t, h)
+        new_wide(2)
+        for g in range(G):
+            for j in range(1, PACK):
+                widen(2, g, j, "s")
+        for tt in (0, 2):
+            s_inter(1, tt)
+            s_inter(1, tt + 1)
+            s_quant(1, tt)
+            s_quant(1, tt + 1)
+        for t in range(4):
+            for h in range(NH):
+                project(1, t, h)
+        for t in range(4):
+            attenuate(1, t, 0)
+        for h in range(NH):
+            h_inter(0, ZH * h, ZH)
+        for h in range(NH):
+            h_quant(0, ZH * h, ZH)
+        for c in range(C):
+            d_sign(c)
+        for g in range(G):
+            widen(2, g, 0, "v")
+        d_inter(0, "s")
+        for t in range(4):
+            attenuate(1, t, 1)
+        d_inter(1, "s")
+        s_inter(2, 0)
+        s_inter(2, 1)
+        s_quant(2, 0)
+        s_quant(2, 1)
+        s_inter(2, 2)
+        s_inter(2, 3)
+        s_quant(2, 2)
+        s_quant(2, 3)
+        for h in range(NH):
+            h_inter(1, ZH * h, ZH)
+        for h in range(NH):
+            h_quant(1, ZH * h, ZH)
+        for t in range(4):
+            project(2, t, 0)
+            attenuate(2, t, 0)
+            project(2, t, 1)
+            attenuate(2, t, 1)
+            if t == 1:
+                d_inter(2, "s")
+        for c in range(C):
+            d_quant(c)
+        for z in range(8):
+            detect(z, (0, 1))
+        for h in range(4):
+            h_inter(2, 256 * h, 256)
+            h_quant(2, 256 * h, 256)
+        for z in range(8):
+            detect(z, (2,))
+            store(z, "s" if z % 2 else "v")

@@ -28,7 +28,7 @@ def tile_tomography_forward_transmission_d3_kernel(tc, F, S_bytes, S_scale, i0, 
     nc = tc.nc
     with ExitStack() as ctx:
         keep = ctx.enter_context(tc.tile_pool(name="keep", bufs=1))
-        fraw_pool = ctx.enter_context(tc.tile_pool(name="fraw", bufs=5))
+        fraw_pool = ctx.enter_context(tc.tile_pool(name="fraw", bufs=6))
         grp = ctx.enter_context(tc.tile_pool(name="grp", bufs=4))
         big = ctx.enter_context(tc.tile_pool(name="big", bufs=4))
         sq = ctx.enter_context(tc.tile_pool(name="sq", bufs=8))
@@ -71,11 +71,10 @@ def tile_tomography_forward_transmission_d3_kernel(tc, F, S_bytes, S_scale, i0, 
             nc.sync.dma_start(out=d_raw[c][:], in_=d_view[c])
 
 
+        i0_flat = i0_t[:].rearrange("p c t -> p (c t)")
         ident = keep.tile([P, P], F32, name="ident")
         make_identity(nc, ident[:])
 
-        i0_flat = i0_t[:].rearrange("p c t -> p (c t)")
-        neg = keep.tile([P, C * PACK], F32, name="neg")
         mag = keep.tile([P, C * PACK], F32, name="mag")
         fac = keep.tile([P, 2, C * PACK], F32, name="fac")
         inv = keep.tile([P, C * PACK], F32, name="inv")
@@ -83,19 +82,27 @@ def tile_tomography_forward_transmission_d3_kernel(tc, F, S_bytes, S_scale, i0, 
         ln_i0 = keep.tile([P, C * PACK], F32, name="ln_i0")
         sgn = keep.tile([P, C * PACK], F32, name="sgn")
 
-        def prep_a():
-            nc.vector.tensor_scalar(out=neg[:], in0=i0_flat, scalar1=-1.0, scalar2=None, op0=ALU.mult)
-            nc.vector.tensor_tensor(out=mag[:], in0=i0_flat, in1=neg[:], op=ALU.max)
-            nc.vector.tensor_scalar(out=mag[:], in0=mag[:], scalar1=2.0**-126, scalar2=None, op0=ALU.max)
-            nc.vector.tensor_scalar(out=fac[:, 0, :], in0=mag[:], scalar1=2.0**-63, scalar2=2.0**64, op0=ALU.max, op1=ALU.min)
-            nc.vector.reciprocal(out=inv[:], in_=fac[:, 0, :])
-            nc.vector.tensor_tensor(out=fac[:, 1, :], in0=mag[:], in1=inv[:], op=ALU.mult)
-            nc.scalar.activation(out=lnf[:], in_=fac[:], func=ACT.Ln)
+        def prepare_i0():
+            nc.gpsimd.tensor_scalar(out=sgn[:], in0=i0_flat, scalar1=0.0, scalar2=2.0, op0=ALU.is_ge, op1=ALU.mult)
+            nc.gpsimd.tensor_scalar(out=sgn[:], in0=sgn[:], scalar1=1.0, scalar2=-1.0, op0=ALU.mult, op1=ALU.add)
+            nc.gpsimd.tensor_tensor(out=mag[:], in0=i0_flat, in1=sgn[:], op=ALU.mult)
+            nc.gpsimd.tensor_scalar(out=mag[:], in0=mag[:], scalar1=2.0**-126, scalar2=1.0, op0=ALU.max, op1=ALU.mult)
+            nc.gpsimd.tensor_scalar(out=fac[:, 0, :], in0=mag[:], scalar1=2.0**-63, scalar2=2.0**64, op0=ALU.max, op1=ALU.min)
 
-        def prep_b():
-            nc.vector.tensor_tensor(out=ln_i0[:], in0=lnf[:, 0, :], in1=lnf[:, 1, :], op=ALU.add)
-            nc.vector.tensor_scalar(out=sgn[:], in0=i0_flat, scalar1=0.0, scalar2=2.0, op0=ALU.is_ge, op1=ALU.mult)
-            nc.vector.tensor_scalar(out=sgn[:], in0=sgn[:], scalar1=-1.0, scalar2=None, op0=ALU.add)
+        def prepare_i0_b():
+            nc.vector.reciprocal(out=inv[:], in_=fac[:, 0, :])
+            nc.gpsimd.tensor_tensor(out=fac[:, 1, :], in0=mag[:], in1=inv[:], op=ALU.mult)
+
+        def log_i0():
+            nc.scalar.activation(out=lnf[:], in_=fac[:], func=ACT.Ln)
+            nc.gpsimd.tensor_tensor(out=ln_i0[:], in0=lnf[:, 0, :], in1=lnf[:, 1, :], op=ALU.add)
+
+        zero = keep.tile([P, 512], BF16, name="zero", align_bytes=64)
+
+        def spin(n):
+            for k in range(n):
+                bank = psum.tile([P, 512], F32, name="bank")
+                nc.tensor.matmul(out=bank[:], lhsT=zero[:, 0:P], rhs=zero[:], start=True, stop=True)
 
         s_wide = {}
 
@@ -190,12 +197,15 @@ def tile_tomography_forward_transmission_d3_kernel(tc, F, S_bytes, S_scale, i0, 
         h_codes = [hq.tile([P, Z], U32, name="h_codes%d" % c, align_bytes=64) for c in range(C)]
         h_scales = [hq.tile([P, Z], U8, name="h_scales%d" % c, align_bytes=64) for c in range(C)]
 
-        def h_inter(c, z0, w):
-            gt = grp.tile([P, 4 * KP], BF16, name="s_grp", align_bytes=64)
+        def h_inter(c, z0, w, eng):
+            gt = grp.tile([P, 4 * 256], BF16, name="h_grp", align_bytes=64)
             h_grp[c, z0] = gt
             src = h_planes[c][:, :, z0 : z0 + w].rearrange("p j (q i) -> p q j i", i=4)
             dst = gt[:, 0 : 4 * w].rearrange("p (q i j) -> p q j i", i=4, j=4)
-            nc.vector.tensor_copy(out=dst, in_=src)
+            if eng == "v":
+                nc.vector.tensor_copy(out=dst, in_=src)
+            else:
+                nc.scalar.copy(out=dst, in_=src)
 
         def h_quant(c, z0, w):
             nc.vector.quantize_mx(
@@ -255,108 +265,104 @@ def tile_tomography_forward_transmission_d3_kernel(tc, F, S_bytes, S_scale, i0, 
                 nc.scalar.copy(out=yt, in_=y_banks[z][:])
             nc.sync.dma_start(out=out[P * z : P * (z + 1), :], in_=yt)
 
+        nc.gpsimd.memset(zero[:], 0.0)
         for g in range(G):
             load_sa(g)
-        for z in range(5):
+        for z in range(8):
             load_f(z)
+            if z % 2:
+                load_sb(z // 2)
+        for c in range(C):
+            load_d(c)
         new_f_grp(0)
         new_wide(0)
         new_f_grp(1)
         new_wide(1)
-        for j in range(PACK):
-            widen(0, 0, j, "s" if j >= 2 else "v")
-        prep_a()
-        for g in range(1, G):
-            for j in range(PACK):
-                widen(0, g, j, "s" if j >= (2 if g < 2 else 3) else "v")
-        prep_b()
-        for z in range(4):
-            f_turn(z)
-        for z in range(5, 8):
-            load_f(z)
+        prepare_i0()
+        spin(6)
         for g in range(G):
-            load_sb(g)
-        for c in range(C):
-            load_d(c)
+            for j in range(PACK):
+                widen(0, g, j, "s" if g < 2 and j >= 2 else "v")
+        prepare_i0_b()
+        for z in range(8):
+            f_turn(z)
+            spin(2 if z < 7 else 0)
+            if z == 0:
+                log_i0()
+            if z % 2:
+                for j in (2, 3):
+                    widen(1, z // 2, j, "s")
         s_inter(0, 0)
         s_inter(0, 1)
         s_quant(0, 0)
-        s_quant(0, 1)
         s_inter(0, 2)
-        for g in range(G):
-            f_quant(0, g)
+        s_quant(0, 1)
         s_inter(0, 3)
         s_quant(0, 2)
-        s_quant(0, 3)
-        for z in range(4, 8):
-            f_turn(z)
-        for t in range(4):
-            project(0, t, 0)
         for g in range(G):
-            for j in range(2):
+            f_quant(0, g)
+            for j in (0, 1):
                 widen(1, g, j, "v")
-        for g in range(G):
-            f_quant(1, g)
-        for t in range(4):
-            project(0, t, 1)
-        for g in range(G):
-            for j in range(2, PACK):
-                widen(1, g, j, "s")
-        for h in range(NH):
-            for t in range(4):
-                attenuate(0, t, h)
+        s_quant(0, 3)
         new_wide(2)
         for g in range(G):
-            for j in range(1, PACK):
+            for j in (2, 3):
                 widen(2, g, j, "s")
-        for tt in (0, 2):
-            s_inter(1, tt)
-            s_inter(1, tt + 1)
-            s_quant(1, tt)
-            s_quant(1, tt + 1)
-        for t in range(4):
-            for h in range(NH):
-                project(1, t, h)
-        for t in range(4):
-            attenuate(1, t, 0)
-        for h in range(NH):
-            h_inter(0, ZH * h, ZH)
-        for h in range(NH):
-            h_quant(0, ZH * h, ZH)
-        for c in range(C):
-            d_sign(c)
         for g in range(G):
-            widen(2, g, 0, "v")
-        d_inter(0, "s")
-        for t in range(4):
-            attenuate(1, t, 1)
-        d_inter(1, "s")
-        s_inter(2, 0)
-        s_inter(2, 1)
-        s_quant(2, 0)
-        s_quant(2, 1)
-        s_inter(2, 2)
-        s_inter(2, 3)
-        s_quant(2, 2)
-        s_quant(2, 3)
+            f_quant(1, g)
         for h in range(NH):
-            h_inter(1, ZH * h, ZH)
-        for h in range(NH):
-            h_quant(1, ZH * h, ZH)
+            for t in range(4):
+                project(0, t, h)
+                attenuate(0, t, h)
+        for g in range(G):
+            for j in (0, 1):
+                widen(2, g, j, "v" if g < 3 else "s")
+        s_inter(1, 0)
+        for k in range(5, 13):
+            c, t = divmod(k, 4)
+            if k < 12:
+                s_inter(c, t)
+            c, t = divmod(k - 1, 4)
+            s_quant(c, t)
+            for h in range(NH):
+                project(c, t, h)
+            if c == 1:
+                h_inter(0, 256 * t, 256, "s" if t < 2 else "s")
+                for h in range(NH):
+                    attenuate(1, t, h)
+            else:
+                h_quant(0, 256 * t, 256)
+            if k == 7:
+                for c in range(C):
+                    d_sign(c)
+                d_inter(0)
+        d_quant(0)
+        for z in range(4):
+            detect(z, (0,))
         for t in range(4):
-            project(2, t, 0)
-            attenuate(2, t, 0)
-            project(2, t, 1)
-            attenuate(2, t, 1)
-            if t == 1:
-                d_inter(2, "s")
-        for c in range(C):
-            d_quant(c)
+            h_inter(1, 256 * t, 256, "s" if t < 2 else "v")
+            for h in range(NH):
+                attenuate(2, t, h)
+        d_inter(1)
+        d_inter(2)
+        d_quant(1)
+        d_quant(2)
+        for t in range(4):
+            h_quant(1, 256 * t, 256)
+        for z in range(4, 8):
+            detect(z, (0,))
         for z in range(8):
-            detect(z, (0, 1))
-        for h in range(4):
-            h_inter(2, 256 * h, 256)
-            h_quant(2, 256 * h, 256)
+            detect(z, (1,))
+        h_inter(2, 0, 256, "v")
+        h_inter(2, 256, 256, "v")
+        h_quant(2, 0, 256)
+        h_inter(2, 512, 256, "v")
+        h_quant(2, 256, 256)
+        h_inter(2, 768, 128, "v")
+        h_quant(2, 512, 256)
+        h_inter(2, 896, 128, "v")
+        h_quant(2, 768, 128)
+        h_quant(2, 896, 128)
         for z in range(8):
             detect(z, (2,))
-            store(z, "s" if z % 2 else "v")
+            store(z, "v" if z in (5, 7) else "s")

@@ -82,27 +82,27 @@ def tile_tomography_forward_transmission_d3_kernel(tc, F, S_bytes, S_scale, i0, 
         ln_i0 = keep.tile([P, C * PACK], F32, name="ln_i0")
         sgn = keep.tile([P, C * PACK], F32, name="sgn")
 
-        def prepare_i0():
-            nc.gpsimd.tensor_scalar(out=sgn[:], in0=i0_flat, scalar1=0.0, scalar2=2.0, op0=ALU.is_ge, op1=ALU.mult)
-            nc.gpsimd.tensor_scalar(out=sgn[:], in0=sgn[:], scalar1=1.0, scalar2=-1.0, op0=ALU.mult, op1=ALU.add)
-            nc.gpsimd.tensor_tensor(out=mag[:], in0=i0_flat, in1=sgn[:], op=ALU.mult)
-            nc.gpsimd.tensor_scalar(out=mag[:], in0=mag[:], scalar1=2.0**-126, scalar2=1.0, op0=ALU.max, op1=ALU.mult)
-            nc.gpsimd.tensor_scalar(out=fac[:, 0, :], in0=mag[:], scalar1=2.0**-63, scalar2=2.0**64, op0=ALU.max, op1=ALU.min)
-
-        def prepare_i0_b():
-            nc.vector.reciprocal(out=inv[:], in_=fac[:, 0, :])
-            nc.gpsimd.tensor_tensor(out=fac[:, 1, :], in0=mag[:], in1=inv[:], op=ALU.mult)
+        def i0_step(k):
+            if k == 0:
+                nc.vector.tensor_scalar(out=sgn[:], in0=i0_flat, scalar1=0.0, scalar2=2.0, op0=ALU.is_ge, op1=ALU.mult)
+            elif k == 1:
+                nc.vector.tensor_scalar(out=sgn[:], in0=sgn[:], scalar1=-1.0, scalar2=None, op0=ALU.add)
+            elif k == 2:
+                nc.vector.tensor_tensor(out=mag[:], in0=i0_flat, in1=sgn[:], op=ALU.mult)
+            elif k == 3:
+                nc.vector.tensor_scalar(out=mag[:], in0=mag[:], scalar1=2.0**-126, scalar2=None, op0=ALU.max)
+            elif k == 4:
+                nc.vector.tensor_scalar(out=fac[:, 0, :], in0=mag[:], scalar1=2.0**-63, scalar2=2.0**64, op0=ALU.max, op1=ALU.min)
+            elif k == 5:
+                nc.vector.reciprocal(out=inv[:], in_=fac[:, 0, :])
+            elif k == 6:
+                nc.vector.tensor_tensor(out=fac[:, 1, :], in0=mag[:], in1=inv[:], op=ALU.mult)
 
         def log_i0():
             nc.scalar.activation(out=lnf[:], in_=fac[:], func=ACT.Ln)
-            nc.gpsimd.tensor_tensor(out=ln_i0[:], in0=lnf[:, 0, :], in1=lnf[:, 1, :], op=ALU.add)
 
-        zero = keep.tile([P, 512], BF16, name="zero", align_bytes=64)
-
-        def spin(n):
-            for k in range(n):
-                bank = psum.tile([P, 512], F32, name="bank")
-                nc.tensor.matmul(out=bank[:], lhsT=zero[:, 0:P], rhs=zero[:], start=True, stop=True)
+        def add_logs():
+            nc.vector.tensor_tensor(out=ln_i0[:], in0=lnf[:, 0, :], in1=lnf[:, 1, :], op=ALU.add)
 
         s_wide = {}
 
@@ -265,30 +265,33 @@ def tile_tomography_forward_transmission_d3_kernel(tc, F, S_bytes, S_scale, i0, 
                 nc.scalar.copy(out=yt, in_=y_banks[z][:])
             nc.sync.dma_start(out=out[P * z : P * (z + 1), :], in_=yt)
 
-        nc.gpsimd.memset(zero[:], 0.0)
         for g in range(G):
             load_sa(g)
-        for z in range(8):
+        for z in range(6):
             load_f(z)
             if z % 2:
                 load_sb(z // 2)
-        for c in range(C):
-            load_d(c)
         new_f_grp(0)
         new_wide(0)
         new_f_grp(1)
         new_wide(1)
-        prepare_i0()
-        spin(6)
+        step = 0
         for g in range(G):
             for j in range(PACK):
-                widen(0, g, j, "s" if g < 2 and j >= 2 else "v")
-        prepare_i0_b()
+                eng = "s" if g < 2 and j >= 2 else "v"
+                widen(0, g, j, eng)
+                if eng == "v" and step < 7:
+                    i0_step(step)
+                    step += 1
+        log_i0()
         for z in range(8):
             f_turn(z)
-            spin(2 if z < 7 else 0)
             if z == 0:
-                log_i0()
+                for k in (6, 7):
+                    load_f(k)
+                load_sb(3)
+                for c in range(C):
+                    load_d(c)
             if z % 2:
                 for j in (2, 3):
                     widen(1, z // 2, j, "s")
@@ -297,23 +300,34 @@ def tile_tomography_forward_transmission_d3_kernel(tc, F, S_bytes, S_scale, i0, 
         s_quant(0, 0)
         s_inter(0, 2)
         s_quant(0, 1)
+        add_logs()
         s_inter(0, 3)
         s_quant(0, 2)
         for g in range(G):
             f_quant(0, g)
-            for j in (0, 1):
-                widen(1, g, j, "v")
+            if g < 3:
+                for j in (0, 1):
+                    widen(1, g, j, "v")
         s_quant(0, 3)
+        for t in range(4):
+            project(0, t, 0)
+            if 8 + t < 8:
+                f_turn(8 + t)
+        for j in (2, 3):
+            widen(1, 3, j, "s")
+        for j in (0, 1):
+            widen(1, 3, j, "v")
         new_wide(2)
         for g in range(G):
             for j in (2, 3):
                 widen(2, g, j, "s")
         for g in range(G):
             f_quant(1, g)
-        for h in range(NH):
-            for t in range(4):
-                project(0, t, h)
-                attenuate(0, t, h)
+        for t in range(4):
+            attenuate(0, t, 0)
+        for t in range(4):
+            project(0, t, 1)
+            attenuate(0, t, 1)
         for g in range(G):
             for j in (0, 1):
                 widen(2, g, j, "v" if g < 3 else "s")
@@ -327,7 +341,7 @@ def tile_tomography_forward_transmission_d3_kernel(tc, F, S_bytes, S_scale, i0, 
             for h in range(NH):
                 project(c, t, h)
             if c == 1:
-                h_inter(0, 256 * t, 256, "s" if t < 2 else "s")
+                h_inter(0, 256 * t, 256, "s")
                 for h in range(NH):
                     attenuate(1, t, h)
             else:

@@ -159,25 +159,31 @@ def tile_tomography_forward_transmission_d3_kernel(tc, F, S_bytes, S_scale, i0, 
                     in_=bank[:].rearrange("p (g u r) -> p g r u", g=2, u=2),
                 )
 
-        def f_quant(h, g):
+        def f_quant(q, g):
+            h, k = divmod(q, 2)
             nc.vector.quantize_mx(
-                out=f_codes[h][:, g, :].bitcast(FP8X4), scales=f_scales[h][:, g, :], in_=f_grp[h][:, g, :].bitcast(BF16)
+                out=f_codes[h][:, g, 256 * k : 256 * (k + 1)].bitcast(FP8X4),
+                scales=f_scales[h][:, g, 256 * k : 256 * (k + 1)],
+                in_=f_grp[h][:, g, 512 * k : 512 * (k + 1)].bitcast(BF16),
             )
 
         h_planes = {}
         banks = {}
 
-        def project(c, t, h):
-            bank = psum.tile([P, 512], F32, name="bank")
-            banks[c, t, h] = bank
+        def project(c, t, h, half=None):
+            if (c, t, h) not in banks:
+                bank_tile = psum.tile([P, 512], F32, name="bank")
+                banks[c, t, h] = bank_tile
+            bank = banks[c, t, h]
+            zs = slice(0, ZH) if half is None else slice(256 * half, 256 * (half + 1))
             for g in range(G):
                 cols = slice(P * g, P * (g + 1))
                 nc.tensor.matmul_mx(
-                    out=bank[:],
+                    out=bank[:, zs],
                     lhsT=s_codes[c, t][:, cols].bitcast(FP8X4),
                     lhsT_scale=s_scales[c, t][:, cols],
-                    rhs=f_codes[h][:, g, :].bitcast(FP8X4),
-                    rhs_scale=f_scales[h][:, g, :],
+                    rhs=f_codes[h][:, g, zs].bitcast(FP8X4),
+                    rhs_scale=f_scales[h][:, g, zs],
                     start=(g == 0),
                     stop=(g == G - 1),
                 )
@@ -265,12 +271,20 @@ def tile_tomography_forward_transmission_d3_kernel(tc, F, S_bytes, S_scale, i0, 
                 nc.scalar.copy(out=yt, in_=y_banks[z][:])
             nc.sync.dma_start(out=out[P * z : P * (z + 1), :], in_=yt)
 
-        for g in range(G):
-            load_sa(g)
-        for z in range(6):
-            load_f(z)
-            if z % 2:
-                load_sb(z // 2)
+        load_sa(0)
+        load_sa(1)
+        load_sa(2)
+        load_sa(3)
+        load_f(0)
+        load_f(1)
+        load_sb(0)
+        load_f(2)
+        load_sb(1)
+        load_f(3)
+        load_sb(2)
+        load_f(4)
+        load_sb(3)
+        load_f(5)
         new_f_grp(0)
         new_wide(0)
         new_f_grp(1)
@@ -278,23 +292,21 @@ def tile_tomography_forward_transmission_d3_kernel(tc, F, S_bytes, S_scale, i0, 
         step = 0
         for g in range(G):
             for j in range(PACK):
-                eng = "s" if g < 2 and j >= 2 else "v"
+                eng = "s" if (g < 2 and j >= 2) or (g == 2 and j == 3) else "v"
                 widen(0, g, j, eng)
                 if eng == "v" and step < 7:
                     i0_step(step)
                     step += 1
         log_i0()
-        for z in range(8):
+        for z in range(4):
             f_turn(z)
             if z == 0:
                 for k in (6, 7):
                     load_f(k)
-                load_sb(3)
                 for c in range(C):
                     load_d(c)
-            if z % 2:
-                for j in (2, 3):
-                    widen(1, z // 2, j, "s")
+            for j in (2, 3):
+                widen(1, z, j, "s")
         s_inter(0, 0)
         s_inter(0, 1)
         s_quant(0, 0)
@@ -302,43 +314,58 @@ def tile_tomography_forward_transmission_d3_kernel(tc, F, S_bytes, S_scale, i0, 
         s_quant(0, 1)
         add_logs()
         s_inter(0, 3)
-        s_quant(0, 2)
         for g in range(G):
             f_quant(0, g)
-            if g < 3:
-                for j in (0, 1):
-                    widen(1, g, j, "v")
+        s_quant(0, 2)
         s_quant(0, 3)
         for t in range(4):
-            project(0, t, 0)
-            if 8 + t < 8:
-                f_turn(8 + t)
-        for j in (2, 3):
-            widen(1, 3, j, "s")
-        for j in (0, 1):
-            widen(1, 3, j, "v")
+            project(0, t, 0, 0)
         new_wide(2)
-        for g in range(G):
+        for g in range(4):
             for j in (2, 3):
                 widen(2, g, j, "s")
+        f_turn(4)
+        f_turn(5)
+        for g in range(G):
+            for j in (0, 1):
+                widen(1, g, j, "v")
         for g in range(G):
             f_quant(1, g)
         for t in range(4):
+            project(0, t, 0, 1)
+        f_turn(6)
+        f_turn(7)
+        s_inter(1, 0)
+        s_inter(1, 1)
+        s_quant(1, 0)
+        for g in range(G):
+            f_quant(2, g)
+        for t in range(4):
             attenuate(0, t, 0)
         for t in range(4):
-            project(0, t, 1)
-            attenuate(0, t, 1)
+            project(0, t, 1, 0)
+        s_inter(1, 2)
+        s_quant(1, 1)
         for g in range(G):
+            f_quant(3, g)
+        for t in range(4):
+            project(0, t, 1, 1)
+        for g in range(4, G):
+            for j in (2, 3):
+                widen(2, g, j, "s")
+        for t in range(4):
+            attenuate(0, t, 1)
+        for g in range(3, G):
             for j in (0, 1):
-                widen(2, g, j, "v" if g < 3 else "s")
-        s_inter(1, 0)
+                widen(2, g, j, "s")
         for k in range(5, 13):
             c, t = divmod(k, 4)
-            if k < 12:
+            if 6 < k < 12:
                 s_inter(c, t)
             c, t = divmod(k - 1, 4)
-            s_quant(c, t)
-            for h in range(NH):
+            if k > 6:
+                s_quant(c, t)
+            for h in range(NH if c == 1 else 1):
                 project(c, t, h)
             if c == 1:
                 h_inter(0, 256 * t, 256, "s")
@@ -347,36 +374,52 @@ def tile_tomography_forward_transmission_d3_kernel(tc, F, S_bytes, S_scale, i0, 
             else:
                 h_quant(0, 256 * t, 256)
             if k == 7:
+                for g in range(3):
+                    for j in (0, 1):
+                        widen(2, g, j, "v")
                 for c in range(C):
                     d_sign(c)
                 d_inter(0)
-        d_quant(0)
-        for z in range(4):
-            detect(z, (0,))
         for t in range(4):
-            h_inter(1, 256 * t, 256, "s" if t < 2 else "v")
-            for h in range(NH):
-                attenuate(2, t, h)
+            project(2, t, 1)
+        for t in range(4):
+            attenuate(2, t, 0)
+        for k in (1, 2, 3):
+            h_inter(1, 256 * k, 256, "s")
+        for t in range(4):
+            attenuate(2, t, 1)
+        for k in (0,):
+            h_inter(1, 256 * k, 256, "v")
+        d_quant(0)
         d_inter(1)
         d_inter(2)
         d_quant(1)
         d_quant(2)
-        for t in range(4):
-            h_quant(1, 256 * t, 256)
-        for z in range(4, 8):
-            detect(z, (0,))
-        for z in range(8):
-            detect(z, (1,))
+        for k in range(2):
+            h_quant(1, 256 * k, 256)
+        for z in range(4):
+            detect(z, (0, 1))
         h_inter(2, 0, 256, "v")
         h_inter(2, 256, 256, "v")
         h_quant(2, 0, 256)
-        h_inter(2, 512, 256, "v")
+        for k in ():
+            h_inter(1, 256 * k, 256, "v")
         h_quant(2, 256, 256)
+        for z in range(4, 8):
+            detect(z, (0,))
+        for z in range(4):
+            detect(z, (2,))
+            store(z, "s")
+        for k in range(2, 4):
+            h_quant(1, 256 * k, 256)
+        for z in range(4, 8):
+            detect(z, (1,))
+        h_inter(2, 512, 256, "v")
         h_inter(2, 768, 128, "v")
         h_quant(2, 512, 256)
         h_inter(2, 896, 128, "v")
         h_quant(2, 768, 128)
         h_quant(2, 896, 128)
-        for z in range(8):
+        for z in range(4, 8):
             detect(z, (2,))
-            store(z, "v" if z in (5, 7) else "s")
+            store(z, "v" if z == 7 else "s")

@@ -28,11 +28,12 @@ def tile_tomography_forward_transmission_d3_kernel(tc, F, S_bytes, S_scale, i0, 
     nc = tc.nc
     with ExitStack() as ctx:
         keep = ctx.enter_context(tc.tile_pool(name="keep", bufs=1))
-        fraw_pool = ctx.enter_context(tc.tile_pool(name="fraw", bufs=6))
+        fraw_pool = ctx.enter_context(tc.tile_pool(name="fraw", bufs=5))
         grp = ctx.enter_context(tc.tile_pool(name="grp", bufs=4))
-        big = ctx.enter_context(tc.tile_pool(name="big", bufs=4))
+        fpool = ctx.enter_context(tc.tile_pool(name="fpool", bufs=3))
+        big = ctx.enter_context(tc.tile_pool(name="big", bufs=3))
         sq = ctx.enter_context(tc.tile_pool(name="sq", bufs=8))
-        hp = ctx.enter_context(tc.tile_pool(name="hp", bufs=2))
+        hp = ctx.enter_context(tc.tile_pool(name="hp", bufs=4))
         hq = ctx.enter_context(tc.tile_pool(name="hq", bufs=1))
         psum = ctx.enter_context(tc.psum_pool(name="psum", bufs=8))
         ctx.enter_context(tc.manual_schedule())
@@ -98,6 +99,13 @@ def tile_tomography_forward_transmission_d3_kernel(tc, F, S_bytes, S_scale, i0, 
             elif k == 6:
                 nc.vector.tensor_tensor(out=fac[:, 1, :], in0=mag[:], in1=inv[:], op=ALU.mult)
 
+        unit = keep.tile([P, 1], F32, name="unit")
+        ln_unit = keep.tile([P, 1], F32, name="ln_unit")
+
+        def load_ln_table():
+            nc.vector.memset(unit[:], 1.0)
+            nc.scalar.activation(out=ln_unit[:], in_=unit[:], func=ACT.Ln)
+
         def log_i0():
             nc.scalar.activation(out=lnf[:], in_=fac[:], func=ACT.Ln)
 
@@ -134,15 +142,17 @@ def tile_tomography_forward_transmission_d3_kernel(tc, F, S_bytes, S_scale, i0, 
 
         f_grp = {}
 
-        def new_f_grp(h):
-            f_grp_tile = big.tile([P, G, ZH * 2], F32, name="big", align_bytes=64)
-            f_grp[h] = f_grp_tile
+        def new_f_grp(q):
+            f_grp_tile = fpool.tile([P, G, ZH], F32, name="f_grp", align_bytes=64)
+            f_grp[q] = f_grp_tile
         f_codes = [keep.tile([P, G, ZH], U32, name="f_codes%d" % h, align_bytes=64) for h in range(NH)]
         f_scales = [keep.tile([P, G, ZH], U8, name="f_scales%d" % h, align_bytes=64) for h in range(NH)]
 
         def f_turn(z):
             words = f_raw[z][:].bitcast(F32)
-            h, zz = divmod(z, 4)
+            q, zz = divmod(z, 2)
+            if zz == 0:
+                new_f_grp(q)
             for gp in range(2):
                 bank = psum.tile([P, 512], F32, name="bank")
                 for k in range(2):
@@ -153,7 +163,7 @@ def tile_tomography_forward_transmission_d3_kernel(tc, F, S_bytes, S_scale, i0, 
                             words[:, 256 * g + u : 256 * (g + 1) : 2],
                             ident[:],
                         )
-                dst = f_grp[h][:, 2 * gp : 2 * gp + 2, 2 * P * zz : 2 * P * (zz + 1)]
+                dst = f_grp[q][:, 2 * gp : 2 * gp + 2, 2 * P * zz : 2 * P * (zz + 1)]
                 nc.scalar.copy(
                     out=dst.rearrange("p g (r u) -> p g r u", u=2),
                     in_=bank[:].rearrange("p (g u r) -> p g r u", g=2, u=2),
@@ -164,7 +174,7 @@ def tile_tomography_forward_transmission_d3_kernel(tc, F, S_bytes, S_scale, i0, 
             nc.vector.quantize_mx(
                 out=f_codes[h][:, g, 256 * k : 256 * (k + 1)].bitcast(FP8X4),
                 scales=f_scales[h][:, g, 256 * k : 256 * (k + 1)],
-                in_=f_grp[h][:, g, 512 * k : 512 * (k + 1)].bitcast(BF16),
+                in_=f_grp[q][:, g, :].bitcast(BF16),
             )
 
         h_planes = {}
@@ -189,10 +199,10 @@ def tile_tomography_forward_transmission_d3_kernel(tc, F, S_bytes, S_scale, i0, 
                 )
 
         def attenuate(c, t, h):
-            if c not in h_planes:
-                h_planes[c] = hp.tile([P, PACK, Z], BF16, name="h_plane", align_bytes=64)
+            if (c, h) not in h_planes:
+                h_planes[c, h] = hp.tile([P, PACK, ZH], BF16, name="h_plane", align_bytes=64)
             nc.scalar.activation(
-                out=h_planes[c][:, t, ZH * h : ZH * (h + 1)],
+                out=h_planes[c, h][:, t, :],
                 in_=banks[c, t, h][:],
                 func=ACT.Exp,
                 bias=ln_i0[:, PACK * c + t : PACK * c + t + 1],
@@ -206,7 +216,8 @@ def tile_tomography_forward_transmission_d3_kernel(tc, F, S_bytes, S_scale, i0, 
         def h_inter(c, z0, w, eng):
             gt = grp.tile([P, 4 * 256], BF16, name="h_grp", align_bytes=64)
             h_grp[c, z0] = gt
-            src = h_planes[c][:, :, z0 : z0 + w].rearrange("p j (q i) -> p q j i", i=4)
+            h, z1 = divmod(z0, ZH)
+            src = h_planes[c, h][:, :, z1 : z1 + w].rearrange("p j (q i) -> p q j i", i=4)
             dst = gt[:, 0 : 4 * w].rearrange("p (q i j) -> p q j i", i=4, j=4)
             if eng == "v":
                 nc.vector.tensor_copy(out=dst, in_=src)
@@ -271,6 +282,7 @@ def tile_tomography_forward_transmission_d3_kernel(tc, F, S_bytes, S_scale, i0, 
                 nc.scalar.copy(out=yt, in_=y_banks[z][:])
             nc.sync.dma_start(out=out[P * z : P * (z + 1), :], in_=yt)
 
+        load_ln_table()
         load_sa(0)
         load_sa(1)
         load_sa(2)
@@ -285,9 +297,7 @@ def tile_tomography_forward_transmission_d3_kernel(tc, F, S_bytes, S_scale, i0, 
         load_f(4)
         load_sb(3)
         load_f(5)
-        new_f_grp(0)
         new_wide(0)
-        new_f_grp(1)
         new_wide(1)
         step = 0
         for g in range(G):
@@ -298,61 +308,65 @@ def tile_tomography_forward_transmission_d3_kernel(tc, F, S_bytes, S_scale, i0, 
                     i0_step(step)
                     step += 1
         log_i0()
-        for z in range(4):
+        for z in range(5):
             f_turn(z)
             if z == 0:
                 for k in (6, 7):
                     load_f(k)
                 for c in range(C):
                     load_d(c)
-            for j in (2, 3):
-                widen(1, z, j, "s")
+            if z < 4:
+                for j in (2, 3):
+                    widen(1, z, j, "s")
         s_inter(0, 0)
         s_inter(0, 1)
         s_quant(0, 0)
         s_inter(0, 2)
         s_quant(0, 1)
         add_logs()
-        s_inter(0, 3)
         for g in range(G):
             f_quant(0, g)
+        s_inter(0, 3)
         s_quant(0, 2)
-        s_quant(0, 3)
-        for t in range(4):
-            project(0, t, 0, 0)
-        new_wide(2)
         for g in range(4):
-            for j in (2, 3):
-                widen(2, g, j, "s")
-        f_turn(4)
-        f_turn(5)
-        for g in range(G):
             for j in (0, 1):
                 widen(1, g, j, "v")
+        s_quant(0, 3)
         for g in range(G):
             f_quant(1, g)
+        for t in range(2):
+            project(0, t, 0, 0)
+        new_wide(2)
+        for g in range(1):
+            for j in (2, 3):
+                widen(2, g, j, "s")
+        for z in range(5, 8):
+            f_turn(z)
+            if True:
+                for j in (2, 3):
+                    widen(2, z - 5 + 1, j, "s")
+        for g in range(4, G):
+            for j in (0, 1):
+                widen(1, g, j, "v")
+        for t in range(2, 4):
+            project(0, t, 0, 0)
         for t in range(4):
             project(0, t, 0, 1)
-        f_turn(6)
-        f_turn(7)
         s_inter(1, 0)
-        s_inter(1, 1)
-        s_quant(1, 0)
         for g in range(G):
             f_quant(2, g)
-        for t in range(4):
-            attenuate(0, t, 0)
-        for t in range(4):
-            project(0, t, 1, 0)
+        s_inter(1, 1)
+        s_quant(1, 0)
         s_inter(1, 2)
         s_quant(1, 1)
         for g in range(G):
             f_quant(3, g)
         for t in range(4):
+            attenuate(0, t, 0)
+        for t in range(4):
+            project(0, t, 1, 0)
+        for t in range(4):
             project(0, t, 1, 1)
-        for g in range(4, G):
-            for j in (2, 3):
-                widen(2, g, j, "s")
         for t in range(4):
             attenuate(0, t, 1)
         for g in range(3, G):
@@ -374,12 +388,13 @@ def tile_tomography_forward_transmission_d3_kernel(tc, F, S_bytes, S_scale, i0, 
             else:
                 h_quant(0, 256 * t, 256)
             if k == 7:
+                for cc in range(C):
+                    d_sign(cc)
+                d_inter(0)
+            if k == 7:
                 for g in range(3):
                     for j in (0, 1):
                         widen(2, g, j, "v")
-                for c in range(C):
-                    d_sign(c)
-                d_inter(0)
         for t in range(4):
             project(2, t, 1)
         for t in range(4):

from contextlib import ExitStack

import concourse.mybir as mybir
from concourse.masks import make_identity

Z, V, R, B = 1024, 2048, 1536, 512
FLOPS = 2 * Z * V * R + 2 * Z * R * B

F32 = mybir.dt.float32
BF16 = mybir.dt.bfloat16
U32 = mybir.dt.uint32
U8 = mybir.dt.uint8
FP8 = mybir.dt.float8_e4m3fn
FP8X4 = mybir.dt.float8_e4m3fn_x4
ALU = mybir.AluOpType
ACT = mybir.ActivationFunctionType

P = 128
PACK = 4
KP = 512
G = V // KP
C = R // KP
ZH = 512
NH = Z // ZH


def tile_tomography_forward_transmission_d3_kernel(tc, F, S_bytes, S_scale, i0, D, out):
    nc = tc.nc
    with ExitStack() as ctx:
        keep = ctx.enter_context(tc.tile_pool(name="keep", bufs=1))
        fraw_pool = ctx.enter_context(tc.tile_pool(name="fraw", bufs=5))
        grp = ctx.enter_context(tc.tile_pool(name="grp", bufs=4))
        fpool = ctx.enter_context(tc.tile_pool(name="fpool", bufs=3))
        big = ctx.enter_context(tc.tile_pool(name="big", bufs=3))
        sq = ctx.enter_context(tc.tile_pool(name="sq", bufs=8))
        hp = ctx.enter_context(tc.tile_pool(name="hp", bufs=4))
        hq = ctx.enter_context(tc.tile_pool(name="hq", bufs=1))
        psum = ctx.enter_context(tc.psum_pool(name="psum", bufs=8))
        ctx.enter_context(tc.manual_schedule())

        scale = keep.tile([P, G, PACK], F32, name="scale")
        i0_t = keep.tile([P, C, PACK], BF16, name="i0_t")
        nc.scalar.dma_start(out=scale[:], in_=S_scale.rearrange("(g p t) o -> p g (t o)", p=P, t=PACK))
        nc.scalar.dma_start(out=i0_t[:], in_=i0.rearrange("(c p t) -> p c t", p=P, t=PACK))
        s_view = S_bytes.rearrange("(g p t) n -> g p t n", p=P, t=PACK)
        sb_a, sb_b = [], []
        for g in range(G):
            a = keep.tile([P, PACK, KP], U8, name="s_bytes_a%d" % g)
            b = keep.tile([P, PACK, 2 * KP], U8, name="s_bytes_b%d" % g)
            sb_a.append(a)
            sb_b.append(b)
        f_raw = {}
        d_raw = []
        for c in range(C):
            dr = keep.tile([P, PACK, B], BF16, name="d_raw%d" % c)
            d_raw.append(dr)

        def load_f(z):
            fr = fraw_pool.tile([P, V], BF16, name="f_raw")
            f_raw[z] = fr
            nc.sync.dma_start(out=fr[:], in_=F[P * z : P * (z + 1), :])

        d_view = D.rearrange("(c p t) b -> c p t b", p=P, t=PACK)

        def load_sa(g):
            nc.sync.dma_start(out=sb_a[g][:], in_=s_view[g][:, :, 0:KP])

        def load_sb(g):
            nc.sync.dma_start(out=sb_b[g][:], in_=s_view[g][:, :, KP:R])

        def load_d(c):
            nc.sync.dma_start(out=d_raw[c][:], in_=d_view[c])


        i0_flat = i0_t[:].rearrange("p c t -> p (c t)")
        ident = keep.tile([P, P], F32, name="ident")
        make_identity(nc, ident[:])

        mag = keep.tile([P, C * PACK], F32, name="mag")
        fac = keep.tile([P, 2, C * PACK], F32, name="fac")
        inv = keep.tile([P, C * PACK], F32, name="inv")
        lnf = keep.tile([P, 2, C * PACK], F32, name="lnf")
        ln_i0 = keep.tile([P, C * PACK], F32, name="ln_i0")
        sgn = keep.tile([P, C * PACK], F32, name="sgn")

        def i0_step(k):
            if k == 0:
                nc.vector.tensor_scalar(out=sgn[:], in0=i0_flat, scalar1=0.0, scalar2=2.0, op0=ALU.is_ge, op1=ALU.mult)
            elif k == 1:
                nc.vector.tensor_scalar(out=sgn[:], in0=sgn[:], scalar1=-1.0, scalar2=None, op0=ALU.add)
            elif k == 2:
                nc.vector.tensor_tensor(out=mag[:], in0=i0_flat, in1=sgn[:], op=ALU.mult)
            elif k == 3:
                nc.vector.tensor_scalar(out=mag[:], in0=mag[:], scalar1=2.0**-126, scalar2=None, op0=ALU.max)
            elif k == 4:
                nc.vector.tensor_scalar(out=fac[:, 0, :], in0=mag[:], scalar1=2.0**-63, scalar2=2.0**64, op0=ALU.max, op1=ALU.min)
            elif k == 5:
                nc.vector.reciprocal(out=inv[:], in_=fac[:, 0, :])
            elif k == 6:
                nc.vector.tensor_tensor(out=fac[:, 1, :], in0=mag[:], in1=inv[:], op=ALU.mult)

        unit = keep.tile([P, 1], F32, name="unit")
        ln_unit = keep.tile([P, 1], F32, name="ln_unit")

        def load_ln_table():
            nc.vector.memset(unit[:], 1.0)
            nc.scalar.activation(out=ln_unit[:], in_=unit[:], func=ACT.Ln)

        def log_i0():
            nc.scalar.activation(out=lnf[:], in_=fac[:], func=ACT.Ln)

        def add_logs():
            nc.vector.tensor_tensor(out=ln_i0[:], in0=lnf[:, 0, :], in1=lnf[:, 1, :], op=ALU.add)

        s_wide = {}

        def new_wide(c):
            wide_tile = big.tile([P, PACK, G * KP], BF16, name="big", align_bytes=64)
            s_wide[c] = wide_tile
        s_grp, s_codes, s_scales = {}, {}, {}

        def widen(c, g, j, eng):
            src = sb_a[g][:, j, :] if c == 0 else sb_b[g][:, j, KP * (c - 1) : KP * c]
            dst = s_wide[c][:, j, KP * g : KP * (g + 1)]
            if eng == "v":
                nc.vector.tensor_scalar(out=dst, in0=src.bitcast(FP8), scalar1=scale[:, g, j : j + 1], scalar2=None, op0=ALU.mult)
            else:
                nc.scalar.activation(out=dst, in_=src.bitcast(FP8), func=ACT.Copy, scale=scale[:, g, j : j + 1])

        def s_inter(c, t):
            gt = grp.tile([P, 4 * KP], BF16, name="s_grp", align_bytes=64)
            s_grp[c, t] = gt
            src = s_wide[c][:].rearrange("p j (q i t) -> p t q j i", i=4, t=4)
            dst = gt[:].rearrange("p (q i j) -> p q j i", i=4, j=4)
            nc.vector.tensor_copy(out=dst, in_=src[:, t])

        def s_quant(c, t):
            co = sq.tile([P, KP], U32, name="s_codes", align_bytes=64)
            sc = sq.tile([P, KP], U8, name="s_scales", align_bytes=64)
            s_codes[c, t], s_scales[c, t] = co, sc
            nc.vector.quantize_mx(out=co[:].bitcast(FP8X4), scales=sc[:], in_=s_grp[c, t][:])

        f_grp = {}

        def new_f_grp(q):
            f_grp_tile = fpool.tile([P, G, ZH], F32, name="f_grp", align_bytes=64)
            f_grp[q] = f_grp_tile
        f_codes = [keep.tile([P, G, ZH], U32, name="f_codes%d" % h, align_bytes=64) for h in range(NH)]
        f_scales = [keep.tile([P, G, ZH], U8, name="f_scales%d" % h, align_bytes=64) for h in range(NH)]

        def f_turn(z):
            words = f_raw[z][:].bitcast(F32)
            q, zz = divmod(z, 2)
            if zz == 0:
                new_f_grp(q)
            for gp in range(2):
                bank = psum.tile([P, 512], F32, name="bank")
                for k in range(2):
                    for u in range(2):
                        g = 2 * gp + k
                        nc.tensor.transpose(
                            bank[:, (2 * k + u) * P : (2 * k + u + 1) * P],
                            words[:, 256 * g + u : 256 * (g + 1) : 2],
                            ident[:],
                        )
                dst = f_grp[q][:, 2 * gp : 2 * gp + 2, 2 * P * zz : 2 * P * (zz + 1)]
                nc.scalar.copy(
                    out=dst.rearrange("p g (r u) -> p g r u", u=2),
                    in_=bank[:].rearrange("p (g u r) -> p g r u", g=2, u=2),
                )

        def f_quant(q, g):
            h, k = divmod(q, 2)
            nc.vector.quantize_mx(
                out=f_codes[h][:, g, 256 * k : 256 * (k + 1)].bitcast(FP8X4),
                scales=f_scales[h][:, g, 256 * k : 256 * (k + 1)],
                in_=f_grp[q][:, g, :].bitcast(BF16),
            )

        h_planes = {}
        banks = {}

        def project(c, t, h, half=None):
            if (c, t, h) not in banks:
                bank_tile = psum.tile([P, 512], F32, name="bank")
                banks[c, t, h] = bank_tile
            bank = banks[c, t, h]
            zs = slice(0, ZH) if half is None else slice(256 * half, 256 * (half + 1))
            for g in range(G):
                cols = slice(P * g, P * (g + 1))
                nc.tensor.matmul_mx(
                    out=bank[:, zs],
                    lhsT=s_codes[c, t][:, cols].bitcast(FP8X4),
                    lhsT_scale=s_scales[c, t][:, cols],
                    rhs=f_codes[h][:, g, zs].bitcast(FP8X4),
                    rhs_scale=f_scales[h][:, g, zs],
                    start=(g == 0),
                    stop=(g == G - 1),
                )

        def attenuate(c, t, h):
            if (c, h) not in h_planes:
                h_planes[c, h] = hp.tile([P, PACK, ZH], BF16, name="h_plane", align_bytes=64)
            nc.scalar.activation(
                out=h_planes[c, h][:, t, :],
                in_=banks[c, t, h][:],
                func=ACT.Exp,
                bias=ln_i0[:, PACK * c + t : PACK * c + t + 1],
                scale=-1.0,
            )

        h_grp = {}
        h_codes = [hq.tile([P, Z], U32, name="h_codes%d" % c, align_bytes=64) for c in range(C)]
        h_scales = [hq.tile([P, Z], U8, name="h_scales%d" % c, align_bytes=64) for c in range(C)]

        def h_inter(c, z0, w, eng):
            gt = grp.tile([P, 4 * 256], BF16, name="h_grp", align_bytes=64)
            h_grp[c, z0] = gt
            h, z1 = divmod(z0, ZH)
            src = h_planes[c, h][:, :, z1 : z1 + w].rearrange("p j (q i) -> p q j i", i=4)
            dst = gt[:, 0 : 4 * w].rearrange("p (q i j) -> p q j i", i=4, j=4)
            if eng == "v":
                nc.vector.tensor_copy(out=dst, in_=src)
            else:
                nc.scalar.copy(out=dst, in_=src)

        def h_quant(c, z0, w):
            nc.vector.quantize_mx(
                out=h_codes[c][:, z0 : z0 + w].bitcast(FP8X4), scales=h_scales[c][:, z0 : z0 + w], in_=h_grp[c, z0][:, 0 : 4 * w]
            )

        d_grp = []
        d_codes = [keep.tile([P, B], U32, name="d_codes%d" % c, align_bytes=64) for c in range(C)]
        d_scales = [keep.tile([P, B], U8, name="d_scales%d" % c, align_bytes=64) for c in range(C)]

        def d_sign(c):
            for j in range(PACK):
                nc.vector.tensor_scalar(
                    out=d_raw[c][:, j, :], in0=d_raw[c][:, j, :], scalar1=sgn[:, PACK * c + j : PACK * c + j + 1], scalar2=None, op0=ALU.mult
                )

        def d_inter(c, eng="v"):
            if not d_grp:
                d_grp_tile = big.tile([P, C, PACK * B], BF16, name="big", align_bytes=64)
                d_grp.append(d_grp_tile)
            dst = d_grp[0][:, c, :].rearrange("p (q i j) -> p q j i", i=4, j=4)
            src = d_raw[c][:].rearrange("p j (q i) -> p q j i", i=4)
            if eng == "v":
                nc.vector.tensor_copy(out=dst, in_=src)
            else:
                nc.scalar.copy(out=dst, in_=src)

        def d_quant(c):
            nc.vector.quantize_mx(out=d_codes[c][:].bitcast(FP8X4), scales=d_scales[c][:], in_=d_grp[0][:, c, :])

        y_banks = {}
        y_all = []

        def detect(z, cs):
            if z not in y_banks:
                y_banks[z] = psum.tile([P, 512], F32, name="bank")
            for c in cs:
                cols = slice(P * z, P * (z + 1))
                nc.tensor.matmul_mx(
                    out=y_banks[z][:],
                    lhsT=h_codes[c][:, cols].bitcast(FP8X4),
                    lhsT_scale=h_scales[c][:, cols],
                    rhs=d_codes[c][:].bitcast(FP8X4),
                    rhs_scale=d_scales[c][:],
                    start=(c == 0),
                    stop=(c == C - 1),
                )

        def store(z, eng):
            if not y_all:
                y_tile = big.tile([P, 8, B], F32, name="big", align_bytes=64)
                y_all.append(y_tile)
            yt = y_all[0][:, z, :]
            if eng == "v":
                nc.vector.tensor_copy(out=yt, in_=y_banks[z][:])
            else:
                nc.scalar.copy(out=yt, in_=y_banks[z][:])
            nc.sync.dma_start(out=out[P * z : P * (z + 1), :], in_=yt)

        load_ln_table()
        load_sa(0)
        load_sa(1)
        load_sa(2)
        load_sa(3)
        load_f(0)
        load_f(1)
        load_sb(0)
        load_f(2)
        load_sb(1)
        load_f(3)
        load_sb(2)
        load_f(4)
        load_sb(3)
        load_f(5)
        new_wide(0)
        new_wide(1)
        step = 0
        for g in range(G):
            for j in range(PACK):
                eng = "s" if (g < 2 and j >= 2) or (g == 2 and j == 3) else "v"
                widen(0, g, j, eng)
                if eng == "v" and step < 7:
                    i0_step(step)
                    step += 1
        log_i0()
        for z in range(5):
            f_turn(z)
            if z == 0:
                for k in (6, 7):
                    load_f(k)
                for c in range(C):
                    load_d(c)
            if z < 4:
                for j in (2, 3):
                    widen(1, z, j, "s")
        s_inter(0, 0)
        s_inter(0, 1)
        s_quant(0, 0)
        s_inter(0, 2)
        s_quant(0, 1)
        add_logs()
        for g in range(G):
            f_quant(0, g)
        s_inter(0, 3)
        s_quant(0, 2)
        for g in range(4):
            for j in (0, 1):
                widen(1, g, j, "v")
        s_quant(0, 3)
        for g in range(G):
            f_quant(1, g)
        for t in range(2):
            project(0, t, 0, 0)
        new_wide(2)
        for g in range(1):
            for j in (2, 3):
                widen(2, g, j, "s")
        for z in range(5, 8):
            f_turn(z)
            if True:
                for j in (2, 3):
                    widen(2, z - 5 + 1, j, "s")
        for g in range(4, G):
            for j in (0, 1):
                widen(1, g, j, "v")
        for t in range(2, 4):
            project(0, t, 0, 0)
        for t in range(4):
            project(0, t, 0, 1)
        s_inter(1, 0)
        for g in range(G):
            f_quant(2, g)
        s_inter(1, 1)
        s_quant(1, 0)
        s_inter(1, 2)
        s_quant(1, 1)
        for g in range(G):
            f_quant(3, g)
        for t in range(4):
            attenuate(0, t, 0)
        for t in range(4):
            project(0, t, 1, 0)
        for t in range(4):
            project(0, t, 1, 1)
        for t in range(4):
            attenuate(0, t, 1)
        for g in range(3, G):
            for j in (0, 1):
                widen(2, g, j, "s")
        for k in range(5, 13):
            c, t = divmod(k, 4)
            if 6 < k < 12:
                s_inter(c, t)
            c, t = divmod(k - 1, 4)
            if k > 6:
                s_quant(c, t)
            for h in range(NH if c == 1 else 1):
                project(c, t, h)
            if c == 1:
                h_inter(0, 256 * t, 256, "s")
                for h in range(NH):
                    attenuate(1, t, h)
            else:
                h_quant(0, 256 * t, 256)
            if k == 7:
                for cc in range(C):
                    d_sign(cc)
                d_inter(0)
            if k == 7:
                for g in range(3):
                    for j in (0, 1):
                        widen(2, g, j, "v")
        for t in range(4):
            project(2, t, 1)
        for t in range(4):
            attenuate(2, t, 0)
        for k in (1, 2, 3):
            h_inter(1, 256 * k, 256, "s")
        for t in range(4):
            attenuate(2, t, 1)
        for k in (0,):
            h_inter(1, 256 * k, 256, "v")
        d_quant(0)
        d_inter(1)
        d_inter(2)
        d_quant(1)
        d_quant(2)
        for k in range(2):
            h_quant(1, 256 * k, 256)
        for z in range(4):
            detect(z, (0, 1))
        h_inter(2, 0, 256, "v")
        h_inter(2, 256, 256, "v")
        h_quant(2, 0, 256)
        for k in ():
            h_inter(1, 256 * k, 256, "v")
        h_quant(2, 256, 256)
        for z in range(4, 8):
            detect(z, (0,))
        for z in range(4):
            detect(z, (2,))
            store(z, "s")
        for k in range(2, 4):
            h_quant(1, 256 * k, 256)
        for z in range(4, 8):
            detect(z, (1,))
        h_inter(2, 512, 256, "v")
        h_inter(2, 768, 128, "v")
        h_quant(2, 512, 256)
        h_inter(2, 896, 128, "v")
        h_quant(2, 768, 128)
        h_quant(2, 896, 128)
        for z in range(4, 8):
            detect(z, (2,))
            store(z, "v" if z == 7 else "s")
